import numpy as np
import ml_dtypes


def mxq(x, axis, fmt="e4m3"):
    dtype, down = {"e4m3": (ml_dtypes.float8_e4m3fn, 7), "e5m2": (ml_dtypes.float8_e5m2, 14)}[fmt]
    v = np.moveaxis(np.asarray(x, np.float32).astype(ml_dtypes.bfloat16).astype(np.float64), axis, -1)
    blocks = v.reshape(v.shape[:-1] + (-1, 32))
    amax = np.abs(blocks).max(-1, keepdims=True)
    byte = np.maximum(np.where(amax > 0, np.frexp(amax)[1] - 1 + 127, 0) - down, 1)
    scale = np.exp2(byte - 127.0)
    codes = (blocks / scale).astype(np.float32).astype(dtype).astype(np.float64)
    return np.moveaxis((codes * scale).reshape(v.shape), -1, axis)


WIDE = False


def mx_kscale(k):
    if not WIDE:
        return np.ones(k)
    levels = np.array([10, -10, 5, -5, 0])
    if k % 512:
        return np.exp2(np.random.permutation(np.resize(levels, k // 32))).repeat(32)
    a = np.empty((k // 512, 16))
    for p in range(k // 512):
        a[p, :8] = np.random.permutation(np.resize(levels, 8))
        for g in range(8):
            far = levels[np.abs(levels - a[p, g]) >= 10]
            a[p, g + 8] = far[np.random.randint(len(far))]
    return np.exp2(a.ravel()).repeat(32)


def f64(x):
    return np.asarray(x).astype(np.float64)


E2M1 = np.array([0.0, 0.5, 1.0, 1.5, 2.0, 3.0, 4.0, 6.0, -0.0, -0.5, -1.0, -1.5, -2.0, -3.0, -4.0, -6.0])


def pack_weight(w, fmt):
    k, n = w.shape
    w = f64(np.asarray(w, np.float32).astype(ml_dtypes.bfloat16)).reshape(k // 32, 32, n)
    amax = np.abs(w).max(1)
    if fmt == "e4m3":
        byte = np.frexp(amax)[1] - 1 + 127 - 7
    else:
        mant, ex = np.frexp(amax / 6.0)
        byte = np.where(mant > 0.5, ex, ex - 1) + 127
    byte = np.clip(np.where(amax > 0, byte, 1), 1, 254)
    scaled = (w * np.exp2(127.0 - byte)[:, None, :]).reshape(k, n).astype(np.float32)
    by_word = np.ascontiguousarray(scaled.reshape(k // 512, 128, 4, n).transpose(0, 1, 3, 2))
    if fmt == "e4m3":
        words = by_word.astype(ml_dtypes.float8_e4m3fn).view(np.uint8)
    else:
        c = by_word.astype(ml_dtypes.float4_e2m1fn).view(np.uint8) & 0xF
        words = (c[..., 0::2] | (c[..., 1::2] << 4)).reshape(k // 512, 128, 2 * n)
    return np.ascontiguousarray(words), np.ascontiguousarray(byte.astype(np.uint8).reshape(k // 512, 16, n))


def unpack_weight(words, scales, fmt):
    g, _, n = scales.shape
    words = np.ascontiguousarray(words).reshape(g, 128, n, -1)
    if fmt == "e4m3":
        vals = words.view(ml_dtypes.float8_e4m3fn).astype(np.float64)
    else:
        nib = np.empty((g, 128, n, 4), np.uint8)
        nib[..., 0::2] = words & 0xF
        nib[..., 1::2] = words >> 4
        vals = E2M1[nib]
    vals = vals * np.repeat(np.exp2(scales.astype(np.float64) - 127.0), 8, axis=1)[..., None]
    return vals.transpose(0, 1, 3, 2).reshape(g * 512, n)


def sigmoid(v):
    return 1.0 / (1.0 + np.exp(-v))


def bf(x):
    return np.asarray(x, np.float32).astype(ml_dtypes.bfloat16)


def planes(Y):
    r, m = Y.shape
    b = f64(bf(Y)).reshape(r // 32, 32, m)
    amax = np.abs(b).max(1)
    byte = np.clip(np.where(amax > 0, np.frexp(amax)[1] - 1 + 127 - 7, 1), 1, 254)
    codes = (b * np.exp2(127.0 - byte)[:, None, :]).reshape(r, m).astype(np.float32).astype(ml_dtypes.float8_e4m3fn).view(np.uint8)
    words = codes.reshape(r // 512, 128, 4, m).transpose(0, 1, 3, 2)
    return np.ascontiguousarray(words), np.ascontiguousarray(byte.astype(np.uint8).reshape(r // 512, 16, m))


K, L, T, B, N = 1024, 512, 1024, 128, 512


def setup_inputs():
    n = np.random.standard_normal
    fk = mx_kscale(K)
    fl = mx_kscale(L)
    xtp = pack_weight(n((K, T)) / fk[:, None], "e2m1")
    wvp = pack_weight(n((K, N)) * 1 / np.sqrt(K) * fk[:, None], "e4m3")
    wqp = pack_weight(n((L, N)) * 1 / np.sqrt(L) * fl[:, None], "e4m3")
    wgp = pack_weight(n((K, N)) * 1 / np.sqrt(K) * fk[:, None], "e2m1")
    return {
        "xt_words": xtp[0],
        "xt_scales": xtp[1],
        "wv_words": wvp[0],
        "wv_scales": wvp[1],
        "xq": (n((L, T)) / fl[:, None]).astype(np.float32),
        "wq_words": wqp[0],
        "wq_scales": wqp[1],
        "wg_words": wgp[0],
        "wg_scales": wgp[1],
        "bw": (np.random.uniform(0.5, 2.0, (1, B))).astype(np.float32),
    }


def reference(xt_words, xt_scales, wv_words, wv_scales, xq, wq_words, wq_scales, wg_words, wg_scales, bw):
    xtu = unpack_weight(xt_words, xt_scales, "e2m1")
    wvu = unpack_weight(wv_words, wv_scales, "e4m3")
    wqu = unpack_weight(wq_words, wq_scales, "e4m3")
    wgu = unpack_weight(wg_words, wg_scales, "e2m1")
    xqq = mxq(f64(xq), 0, "e4m3")
    v = wvu.T @ xtu + wqu.T @ xqq
    g = wgu.T @ xtu
    s = sigmoid(g)
    num = (s * v).reshape(N, B, T // B).sum(axis=2)
    den = s.reshape(N, B, T // B).sum(axis=2)
    y = f64(bw) * num / (den + 0.1)
    words, scales = planes(y)
    return y, words, scales

@@ -1,0 +1,317 @@
+from contextlib import ExitStack
+
+import concourse.mybir as mybir
+from concourse.masks import make_identity
+
+K, L, T, B, N = 1024, 512, 1024, 128, 512
+FLOPS = 2 * N * T * (K + L + K)
+
+F32 = mybir.dt.float32
+BF16 = mybir.dt.bfloat16
+I32 = mybir.dt.int32
+U32 = mybir.dt.uint32
+U8 = mybir.dt.uint8
+FP8X4 = mybir.dt.float8_e4m3fn_x4
+FP4X4 = mybir.dt.float4_e2m1fn_x4
+ACT = mybir.ActivationFunctionType
+ALU = mybir.AluOpType
+AXIS = mybir.AxisListType
+
+P = 128
+PACK = 4
+K_PASSES = K // (P * PACK)
+GROUP = T // B
+N_TILES = N // P
+HALVES = 2
+T_HALF = T // HALVES
+B_HALF = B // HALVES
+QUARTERS = 4
+T_QUARTER = T // QUARTERS
+TILES = HALVES * N_TILES
+QUADS = 4
+SUMMED = 2
+
+
+def tile_mix_gated_mean_of_neighbours_pl_kernel(
+    tc, xt_words, xt_scales, wv_words, wv_scales, xq, wq_words, wq_scales, wg_words, wg_scales, bw,
+    out_0, out_1, out_2,
+):
+    nc = tc.nc
+    with ExitStack() as ctx:
+        sb = ctx.enter_context(tc.tile_pool(name="sb", bufs=1))
+        ps = ctx.enter_context(tc.psum_pool(name="ps", bufs=1))
+        ctx.enter_context(tc.manual_schedule())
+
+        def sbuf(name, shape, dtype):
+            return sb.tile(shape, dtype, name=name, align_bytes=64)
+
+        banks = [ps.tile([P, T_HALF], F32, name="bank%d" % k) for k in range(TILES)]
+
+        xt_w = sbuf("xt_w", [P, K_PASSES, 2 * T], U8)
+        wg_w = sbuf("wg_w", [P, K_PASSES, 2 * N], U8)
+        wv_w = sbuf("wv_w", [P, K_PASSES, N], U32)
+        wq_w = sbuf("wq_w", [P, N], U32)
+        xt_s = sbuf("xt_s", [P, K_PASSES, T], U8)
+        wg_s = sbuf("wg_s", [P, K_PASSES, N], U8)
+        wv_s = sbuf("wv_s", [P, K_PASSES, N], U8)
+        wq_s = sbuf("wq_s", [P, 1, N], U8)
+        xq_raw = [sbuf("xq_raw%d" % q, [P, PACK, T_QUARTER], F32) for q in range(QUARTERS)]
+        xq_bf = [sbuf("xq_bf%d" % q, [P, T_QUARTER, PACK], BF16) for q in range(QUARTERS)]
+        xq_w = [sbuf("xq_w%d" % h, [P, T_HALF], U32) for h in range(HALVES)]
+        xq_s = [sbuf("xq_s%d" % h, [P, T_HALF], U8) for h in range(HALVES)]
+        bw_col = sbuf("bw_col", [B, 1], F32)
+        ident = sbuf("ident", [P, P], F32)
+        gates = [sbuf("gates%d" % k, [P, T_HALF], F32) for k in range(TILES)]
+        gated = {k: sbuf("gated%d" % k, [P, T_HALF], F32) for k in range(TILES) if k % N_TILES < SUMMED}
+        stacked = {m: sbuf("stacked%d" % m, [P, GROUP, B], F32) for m in range(SUMMED, N_TILES)}
+        folded = [sbuf("folded%d" % k, [P, T_HALF // 2], F32) for k in range(2 * TILES)]
+        den = sbuf("den", [P, N_TILES, B], F32)
+        num = sbuf("num", [P, SUMMED, B], F32)
+        root = sbuf("root", [P, N_TILES, B], F32)
+        inv = sbuf("inv", [P, N_TILES, B], F32)
+        mean = sbuf("mean", [P, SUMMED, B], F32)
+        inv_rows = sbuf("inv_rows", [B, (N_TILES - SUMMED) * P], F32)
+        y_rows = sbuf("y_rows", [B, PACK, P], F32)
+        y = sbuf("y", [P, PACK * B], F32)
+        y_bf = sbuf("y_bf", [P, B, PACK], BF16)
+        y_w = sbuf("y_w", [P, B], U32)
+        y_s = sbuf("y_s", [P, B], U8)
+
+        def flat_words(plane):
+            return plane[:].rearrange("p z c -> p (z c)").bitcast(I32)
+
+        def load_scales(queue, plane, scales, quad):
+            queue.dma_start(
+                out=plane[32 * quad : 32 * quad + 4, :, :].bitcast(I32),
+                in_=scales[:, 4 * quad : 4 * quad + 4, :].rearrange("z r c -> r z c").bitcast(I32),
+            )
+
+        xq_rows = xq.rearrange("(p j) t -> p j t", j=PACK)
+
+        def load_xq(q):
+            nc.sync.dma_start(out=xq_raw[q][:], in_=xq_rows[:, :, q * T_QUARTER : (q + 1) * T_QUARTER])
+
+        for plane in (xt_s, wg_s, wv_s, wq_s):
+            nc.vector.memset(flat_words(plane), 0)
+        warm = sbuf("warm", [P, 2], F32)
+        nc.vector.memset(warm[:, 0:1], 0.0)
+        nc.scalar.activation(out=warm[:, 1:2], in_=warm[:, 0:1], func=ACT.Sigmoid)
+
+        nc.gpsimd.dma_start(out=wg_w[:].bitcast(I32), in_=wg_words.rearrange("z p c -> p z c").bitcast(I32))
+        load_scales(nc.gpsimd, wg_s, wg_scales, QUADS - 1)
+        nc.sync.dma_start(out=xt_w[:].bitcast(I32), in_=xt_words.rearrange("z p c -> p z c").bitcast(I32))
+        for quad in range(QUADS):
+            load_scales(nc.sync, xt_s, xt_scales, quad)
+        for quad in range(QUADS - 1):
+            load_scales(nc.sync, wg_s, wg_scales, quad)
+        load_xq(0)
+        for quad in range(QUADS):
+            load_scales(nc.sync, wv_s, wv_scales, quad)
+        load_xq(1)
+        nc.sync.dma_start(
+            out=wv_w[:].bitcast(I32), in_=wv_words.rearrange("z p n r -> p z (n r)").bitcast(I32)
+        )
+        nc.sync.dma_start(out=wq_w[:].bitcast(I32), in_=wq_words[0].rearrange("p n r -> p (n r)").bitcast(I32))
+        for quad in range(QUADS):
+            load_scales(nc.sync, wq_s, wq_scales, quad)
+        load_xq(2)
+        load_xq(3)
+        nc.sync.dma_start(out=bw_col[:], in_=bw.rearrange("o b -> b o"))
+        make_identity(nc, ident[:])
+
+        def round_xq(q, copy):
+            copy(
+                out=xq_bf[q][:].rearrange("p (c i) j -> p c j i", i=4),
+                in_=xq_raw[q][:].rearrange("p j (c i) -> p c j i", i=4),
+            )
+
+        def quantise_xq(q):
+            h, part = divmod(q, 2)
+            cols = slice(part * T_QUARTER, (part + 1) * T_QUARTER)
+            nc.vector.quantize_mx(
+                out=xq_w[h][:, cols].bitcast(FP8X4),
+                scales=xq_s[h][:, cols],
+                in_=xq_bf[q][:].rearrange("p t j -> p (t j)"),
+            )
+
+        def bank_order(k):
+            if k % N_TILES < SUMMED:
+                return banks[k][:].rearrange("p (b u j) -> p u b j", u=2, j=GROUP // 2)
+            return banks[k][:].rearrange("p (b j) -> p j b", j=GROUP)
+
+        def tile_order(t, k):
+            if k % N_TILES < SUMMED:
+                return t[:].rearrange("p (u b j) -> p u b j", u=2, j=GROUP // 2)
+            return t[:].rearrange("p (j b) -> p j b", j=GROUP)
+
+        def xt_operand(z, h):
+            return (
+                xt_w[:, z, 2 * h * T_HALF : 2 * (h + 1) * T_HALF].bitcast(FP4X4),
+                xt_s[:, z, h * T_HALF : (h + 1) * T_HALF],
+            )
+
+        def gate(k):
+            h, m = divmod(k, N_TILES)
+            for z in range(K_PASSES):
+                codes, scales = xt_operand(z, h)
+                nc.tensor.matmul_mx(
+                    out=banks[k][:],
+                    lhsT=wg_w[:, z, 2 * m * P : 2 * (m + 1) * P].bitcast(FP4X4),
+                    lhsT_scale=wg_s[:, z, m * P : (m + 1) * P],
+                    rhs=codes,
+                    rhs_scale=scales,
+                    start=(z == 0),
+                    stop=(z == K_PASSES - 1),
+                )
+            nc.scalar.activation(out=tile_order(gates[k], k), in_=bank_order(k), func=ACT.Sigmoid)
+
+        def value(k):
+            h, m = divmod(k, N_TILES)
+            cols = slice(m * P, (m + 1) * P)
+            for z in range(K_PASSES):
+                codes, scales = xt_operand(z, h)
+                nc.tensor.matmul_mx(
+                    out=banks[k][:],
+                    lhsT=wv_w[:, z, cols].bitcast(FP8X4),
+                    lhsT_scale=wv_s[:, z, cols],
+                    rhs=codes,
+                    rhs_scale=scales,
+                    start=(z == 0),
+                    stop=False,
+                )
+            nc.tensor.matmul_mx(
+                out=banks[k][:],
+                lhsT=wq_w[:, cols].bitcast(FP8X4),
+                lhsT_scale=wq_s[:, 0, cols],
+                rhs=xq_w[h][:].bitcast(FP8X4),
+                rhs_scale=xq_s[h][:],
+                start=False,
+                stop=True,
+            )
+            if m < SUMMED:
+                products = tile_order(gated[k], k)
+            else:
+                products = stacked[m][:, :, h * B_HALF : (h + 1) * B_HALF]
+            nc.vector.tensor_tensor(out=products, in0=bank_order(k), in1=tile_order(gates[k], k), op=ALU.mult)
+
+        def groups(total, k):
+            h, m = divmod(k, N_TILES)
+            return total[:, m, h * B_HALF : (h + 1) * B_HALF]
+
+        def sum_whole(total, terms, k):
+            nc.vector.tensor_reduce(
+                out=groups(total, k),
+                in_=terms[k][:].rearrange("p (u b j) -> p b u j", u=2, j=GROUP // 2),
+                axis=AXIS.XY,
+                op=ALU.add,
+            )
+
+        def fold(terms, k, slot):
+            nc.gpsimd.tensor_tensor(
+                out=folded[slot][:], in0=terms[k][:, : T_HALF // 2], in1=terms[k][:, T_HALF // 2 :], op=ALU.add
+            )
+
+        def sum_folded(total, k, slot):
+            pattern = "p (b j) -> p b j" if k % N_TILES < SUMMED else "p (j b) -> p b j"
+            nc.vector.tensor_reduce(
+                out=groups(total, k),
+                in_=folded[slot][:].rearrange(pattern, j=GROUP // 2),
+                axis=AXIS.X,
+                op=ALU.add,
+            )
+
+        def dealt(m0, m1):
+            return y_rows[:, :, 32 * m0 : 32 * m1]
+
+        def deal(ap):
+            return ap.rearrange("b (p i) -> b i p", i=PACK)
+
+        def stack_sum(bank, m):
+            for j in range(GROUP):
+                nc.tensor.matmul(
+                    out=bank[:, :P], lhsT=stacked[m][:, j, :], rhs=ident[:], is_transpose=True,
+                    start=(j == 0), stop=(j == GROUP - 1),
+                )
+            nc.vector.scalar_tensor_tensor(
+                out=dealt(m, m + 1),
+                in0=deal(bank[:, :P]),
+                scalar=bw_col[:],
+                in1=deal(inv_rows[:, (m - SUMMED) * P : (m - SUMMED + 1) * P]),
+                op0=ALU.mult,
+                op1=ALU.mult,
+            )
+
+        for q in range(2):
+            nc.gpsimd.tensor_scalar(
+                out=xq_bf[q][:], in0=xq_raw[q][:].rearrange("p j t -> p t j"),
+                scalar1=1.0, scalar2=0.0, op0=ALU.mult, op1=ALU.add,
+            )
+        for k in range(2):
+            gate(k)
+            sum_whole(den, gates, k)
+        quantise_xq(0)
+        for k in range(2, 4):
+            gate(k)
+            fold(gates, k, k)
+        gate(4)
+        sum_whole(den, gates, 4)
+        quantise_xq(1)
+        gate(5)
+        sum_whole(den, gates, 5)
+        gate(6)
+        fold(gates, 6, 6)
+        round_xq(2, nc.scalar.copy)
+        value(0)
+        sum_folded(den, 2, 2)
+        gate(7)
+        fold(gates, 7, 7)
+        fold(gated, 0, TILES)
+        round_xq(3, nc.scalar.copy)
+        value(1)
+        fold(gated, 1, TILES + 1)
+        sum_folded(den, 3, 3)
+        quantise_xq(2)
+        value(2)
+        sum_folded(den, 6, 6)
+        sum_folded(den, 7, 7)
+        nc.scalar.activation(out=root[:], in_=den[:], func=ACT.Abs_reciprocal_sqrt, bias=0.1)
+        nc.scalar.activation(out=inv[:], in_=root[:], func=ACT.Square)
+        quantise_xq(3)
+        value(3)
+        sum_folded(num, 0, TILES)
+        value(4)
+        fold(gated, 4, TILES + 4)
+        sum_folded(num, 1, TILES + 1)
+        value(5)
+        sum_folded(num, 4, TILES + 4)
+        sum_whole(num, gated, 5)
+        value(6)
+        nc.vector.tensor_tensor(out=mean[:], in0=num[:], in1=inv[:, :SUMMED, :], op=ALU.mult)
+        value(7)
+        for m in range(SUMMED, N_TILES):
+            nc.tensor.transpose(banks[0][:, m * P : (m + 1) * P], inv[:, m, :], ident[:])
+        for m in range(SUMMED):
+            nc.tensor.transpose(banks[0][:, m * P : (m + 1) * P], mean[:, m, :], ident[:])
+        nc.scalar.copy(out=inv_rows[:], in_=banks[0][:, SUMMED * P :])
+        nc.scalar.activation(
+            out=dealt(0, SUMMED), in_=deal(banks[0][:, : SUMMED * P]), func=ACT.Copy, scale=bw_col[:]
+        )
+        for m in range(SUMMED, N_TILES):
+            stack_sum(banks[m - 1], m)
+
+        for bank in (banks[3], banks[4]):
+            for i in range(PACK):
+                nc.tensor.transpose(bank[:, i * B : (i + 1) * B], y_rows[:, i, :], ident[:])
+        nc.vector.tensor_copy(out=y_bf[:], in_=banks[3][:].rearrange("p (i b) -> p b i", i=PACK))
+        nc.scalar.copy(out=y[:], in_=banks[4][:])
+        nc.sync.dma_start(out=out_0.rearrange("(p i) b -> p (i b)", i=PACK), in_=y[:])
+        nc.vector.quantize_mx(
+            out=y_w[:].bitcast(FP8X4), scales=y_s[:], in_=y_bf[:].rearrange("p b r -> p (b r)")
+        )
+        nc.sync.dma_start(out=out_1[0].rearrange("p c r -> p (c r)").bitcast(I32), in_=y_w[:].bitcast(I32))
+        for quad in range(QUADS):
+            queue = nc.scalar if quad % 2 == 0 else nc.sync
+            queue.dma_start(
+                out=out_2[0, 4 * quad : 4 * quad + 4, :].bitcast(I32),
+                in_=y_s[32 * quad : 32 * quad + 4, :].bitcast(I32),
+            )

@@ -47,7 +47,7 @@ def tile_mix_gated_mean_of_neighbours_pl_kernel(
 
         banks = [ps.tile([P, T_HALF], F32, name="bank%d" % k) for k in range(TILES)]
 
-        xt_w = sbuf("xt_w", [P, K_PASSES, 2 * T], U8)
+        xt_w = [sbuf("xt_w%d" % h, [P, K_PASSES, 2 * T_HALF], U8) for h in range(HALVES)]
         wg_w = sbuf("wg_w", [P, K_PASSES, 2 * N], U8)
         wv_w = sbuf("wv_w", [P, K_PASSES, N], U32)
         wq_w = sbuf("wq_w", [P, N], U32)
@@ -56,7 +56,7 @@ def tile_mix_gated_mean_of_neighbours_pl_kernel(
         wv_s = sbuf("wv_s", [P, K_PASSES, N], U8)
         wq_s = sbuf("wq_s", [P, 1, N], U8)
         xq_raw = [sbuf("xq_raw%d" % q, [P, PACK, T_QUARTER], F32) for q in range(QUARTERS)]
-        xq_bf = [sbuf("xq_bf%d" % q, [P, T_QUARTER, PACK], BF16) for q in range(QUARTERS)]
+        xq_bf = [sbuf("xq_bf%d" % h, [P, T_HALF, PACK], BF16) for h in range(HALVES)]
         xq_w = [sbuf("xq_w%d" % h, [P, T_HALF], U32) for h in range(HALVES)]
         xq_s = [sbuf("xq_s%d" % h, [P, T_HALF], U8) for h in range(HALVES)]
         bw_col = sbuf("bw_col", [B, 1], F32)
@@ -70,9 +70,10 @@ def tile_mix_gated_mean_of_neighbours_pl_kernel(
         root = sbuf("root", [P, N_TILES, B], F32)
         inv = sbuf("inv", [P, N_TILES, B], F32)
         mean = sbuf("mean", [P, SUMMED, B], F32)
-        inv_rows = sbuf("inv_rows", [B, (N_TILES - SUMMED) * P], F32)
-        y_rows = sbuf("y_rows", [B, PACK, P], F32)
-        y = sbuf("y", [P, PACK * B], F32)
+        factor_rows = sbuf("factor_rows", [B, (N_TILES - SUMMED) * P], F32)
+        y_rows = sbuf("y_rows", [B, N], F32)
+        y_pairs = sbuf("y_pairs", [B, 2, P, 2], BF16)
+        y = sbuf("y", [P, 2, 2 * B], F32)
         y_bf = sbuf("y_bf", [P, B, PACK], BF16)
         y_w = sbuf("y_w", [P, B], U32)
         y_s = sbuf("y_s", [P, B], U8)
@@ -91,29 +92,35 @@ def tile_mix_gated_mean_of_neighbours_pl_kernel(
         def load_xq(q):
             nc.sync.dma_start(out=xq_raw[q][:], in_=xq_rows[:, :, q * T_QUARTER : (q + 1) * T_QUARTER])
 
-        for plane in (xt_s, wg_s, wv_s, wq_s):
+        for plane in (wg_s, xt_s, wq_s, wv_s):
             nc.vector.memset(flat_words(plane), 0)
         warm = sbuf("warm", [P, 2], F32)
         nc.vector.memset(warm[:, 0:1], 0.0)
         nc.scalar.activation(out=warm[:, 1:2], in_=warm[:, 0:1], func=ACT.Sigmoid)
 
+        def load_xt(h):
+            cols = slice(2 * h * T_HALF, 2 * (h + 1) * T_HALF)
+            nc.sync.dma_start(out=xt_w[h][:].bitcast(I32), in_=xt_words.rearrange("z p c -> p z c")[:, :, cols].bitcast(I32))
+
         nc.gpsimd.dma_start(out=wg_w[:].bitcast(I32), in_=wg_words.rearrange("z p c -> p z c").bitcast(I32))
-        load_scales(nc.gpsimd, wg_s, wg_scales, QUADS - 1)
-        nc.sync.dma_start(out=xt_w[:].bitcast(I32), in_=xt_words.rearrange("z p c -> p z c").bitcast(I32))
+        for quad in range(QUADS):
+            load_scales(nc.gpsimd, wq_s, wq_scales, quad)
+        for quad in range(2):
+            load_scales(nc.sync, wg_s, wg_scales, quad)
+        load_xt(0)
         for quad in range(QUADS):
             load_scales(nc.sync, xt_s, xt_scales, quad)
-        for quad in range(QUADS - 1):
+        for quad in range(2, QUADS):
             load_scales(nc.sync, wg_s, wg_scales, quad)
         load_xq(0)
-        for quad in range(QUADS):
-            load_scales(nc.sync, wv_s, wv_scales, quad)
         load_xq(1)
+        load_xt(1)
         nc.sync.dma_start(
             out=wv_w[:].bitcast(I32), in_=wv_words.rearrange("z p n r -> p z (n r)").bitcast(I32)
         )
-        nc.sync.dma_start(out=wq_w[:].bitcast(I32), in_=wq_words[0].rearrange("p n r -> p (n r)").bitcast(I32))
         for quad in range(QUADS):
-            load_scales(nc.sync, wq_s, wq_scales, quad)
+            load_scales(nc.sync, wv_s, wv_scales, quad)
+        nc.sync.dma_start(out=wq_w[:].bitcast(I32), in_=wq_words[0].rearrange("p n r -> p (n r)").bitcast(I32))
         load_xq(2)
         load_xq(3)
         nc.sync.dma_start(out=bw_col[:], in_=bw.rearrange("o b -> b o"))
@@ -121,17 +128,15 @@ def tile_mix_gated_mean_of_neighbours_pl_kernel(
 
         def round_xq(q, copy):
             copy(
-                out=xq_bf[q][:].rearrange("p (c i) j -> p c j i", i=4),
+                out=xq_bf[q // 2][:, (q % 2) * T_QUARTER : (q % 2 + 1) * T_QUARTER, :].rearrange(
+                    "p (c i) j -> p c j i", i=4
+                ),
                 in_=xq_raw[q][:].rearrange("p j (c i) -> p c j i", i=4),
             )
 
-        def quantise_xq(q):
-            h, part = divmod(q, 2)
-            cols = slice(part * T_QUARTER, (part + 1) * T_QUARTER)
+        def quantise_xq(h):
             nc.vector.quantize_mx(
-                out=xq_w[h][:, cols].bitcast(FP8X4),
-                scales=xq_s[h][:, cols],
-                in_=xq_bf[q][:].rearrange("p t j -> p (t j)"),
+                out=xq_w[h][:].bitcast(FP8X4), scales=xq_s[h][:], in_=xq_bf[h][:].rearrange("p t j -> p (t j)")
             )
 
         def bank_order(k):
@@ -146,7 +151,7 @@ def tile_mix_gated_mean_of_neighbours_pl_kernel(
 
         def xt_operand(z, h):
             return (
-                xt_w[:, z, 2 * h * T_HALF : 2 * (h + 1) * T_HALF].bitcast(FP4X4),
+                xt_w[h][:, z, :].bitcast(FP4X4),
                 xt_s[:, z, h * T_HALF : (h + 1) * T_HALF],
             )
 
@@ -165,7 +170,7 @@ def tile_mix_gated_mean_of_neighbours_pl_kernel(
                 )
             nc.scalar.activation(out=tile_order(gates[k], k), in_=bank_order(k), func=ACT.Sigmoid)
 
-        def value(k):
+        def value_xt(k):
             h, m = divmod(k, N_TILES)
             cols = slice(m * P, (m + 1) * P)
             for z in range(K_PASSES):
@@ -179,6 +184,10 @@ def tile_mix_gated_mean_of_neighbours_pl_kernel(
                     start=(z == 0),
                     stop=False,
                 )
+
+        def value_xq(k):
+            h, m = divmod(k, N_TILES)
+            cols = slice(m * P, (m + 1) * P)
             nc.tensor.matmul_mx(
                 out=banks[k][:],
                 lhsT=wq_w[:, cols].bitcast(FP8X4),
@@ -193,6 +202,10 @@ def tile_mix_gated_mean_of_neighbours_pl_kernel(
             else:
                 products = stacked[m][:, :, h * B_HALF : (h + 1) * B_HALF]
             nc.vector.tensor_tensor(out=products, in0=bank_order(k), in1=tile_order(gates[k], k), op=ALU.mult)
+
+        def value(k):
+            value_xt(k)
+            value_xq(k)
 
         def groups(total, k):
             h, m = divmod(k, N_TILES)
@@ -221,10 +234,10 @@ def tile_mix_gated_mean_of_neighbours_pl_kernel(
             )
 
         def dealt(m0, m1):
-            return y_rows[:, :, 32 * m0 : 32 * m1]
+            return y_pairs[:, :, 32 * m0 : 32 * m1, :]
 
         def deal(ap):
-            return ap.rearrange("b (p i) -> b i p", i=PACK)
+            return ap.rearrange("b (p u e) -> b u p e", u=2, e=2)
 
         def stack_sum(bank, m):
             for j in range(GROUP):
@@ -232,79 +245,96 @@ def tile_mix_gated_mean_of_neighbours_pl_kernel(
                     out=bank[:, :P], lhsT=stacked[m][:, j, :], rhs=ident[:], is_transpose=True,
                     start=(j == 0), stop=(j == GROUP - 1),
                 )
-            nc.vector.scalar_tensor_tensor(
-                out=dealt(m, m + 1),
-                in0=deal(bank[:, :P]),
-                scalar=bw_col[:],
-                in1=deal(inv_rows[:, (m - SUMMED) * P : (m - SUMMED + 1) * P]),
-                op0=ALU.mult,
-                op1=ALU.mult,
+
+        def finish_stack(bank, m):
+            factor = factor_rows[:, (m - SUMMED) * P : (m - SUMMED + 1) * P]
+            nc.vector.tensor_tensor(out=dealt(m, m + 1), in0=deal(bank[:, :P]), in1=deal(factor), op=ALU.mult)
+            nc.vector.tensor_tensor(out=y_rows[:, m * P : (m + 1) * P], in0=bank[:, :P], in1=factor, op=ALU.mult)
+
+        def finish_mean(bank, m):
+            nc.tensor.transpose(bank[:, :P], mean[:, m, :], ident[:])
+            nc.scalar.activation(out=dealt(m, m + 1), in_=deal(bank[:, :P]), func=ACT.Copy, scale=bw_col[:])
+            nc.scalar.activation(out=y_rows[:, m * P : (m + 1) * P], in_=bank[:, :P], func=ACT.Copy, scale=bw_col[:])
+
+        def store_rows(bank, first):
+            for slot in range(2):
+                m = first + 2 * slot
+                nc.tensor.transpose(bank[:, slot * B : (slot + 1) * B], y_rows[:, m * P : (m + 1) * P], ident[:])
+            nc.scalar.copy(out=y[:, first, :], in_=bank[:, : 2 * B])
+            nc.scalar.dma_start(
+                out=out_0.rearrange("(s f p) b -> p f s b", s=2, p=P)[:, first, :, :],
+                in_=y[:, first, :].rearrange("p (s b) -> p s b", s=2),
             )
 
-        for q in range(2):
-            nc.gpsimd.tensor_scalar(
-                out=xq_bf[q][:], in0=xq_raw[q][:].rearrange("p j t -> p t j"),
-                scalar1=1.0, scalar2=0.0, op0=ALU.mult, op1=ALU.add,
-            )
-        for k in range(2):
-            gate(k)
-            sum_whole(den, gates, k)
+        def divide(m):
+            nc.vector.tensor_tensor(out=mean[:, m, :], in0=num[:, m, :], in1=inv[:, m, :], op=ALU.mult)
+
+        round_xq(0, nc.vector.tensor_copy)
+        gate(0)
+        sum_whole(den, gates, 0)
+        round_xq(1, nc.vector.tensor_copy)
+        gate(1)
+        sum_whole(den, gates, 1)
         quantise_xq(0)
-        for k in range(2, 4):
-            gate(k)
-            fold(gates, k, k)
+        gate(2)
+        fold(gates, 2, 2)
+        gate(3)
+        fold(gates, 3, 3)
         gate(4)
         sum_whole(den, gates, 4)
-        quantise_xq(1)
         gate(5)
+        sum_folded(den, 2, 2)
         sum_whole(den, gates, 5)
         gate(6)
         fold(gates, 6, 6)
-        round_xq(2, nc.scalar.copy)
-        value(0)
-        sum_folded(den, 2, 2)
         gate(7)
         fold(gates, 7, 7)
-        fold(gated, 0, TILES)
-        round_xq(3, nc.scalar.copy)
-        value(1)
-        fold(gated, 1, TILES + 1)
         sum_folded(den, 3, 3)
-        quantise_xq(2)
-        value(2)
+        round_xq(2, nc.scalar.copy)
+        round_xq(3, nc.scalar.copy)
+        value(0)
+        fold(gated, 0, 0)
         sum_folded(den, 6, 6)
+        value(1)
         sum_folded(den, 7, 7)
+        value(2)
+        quantise_xq(1)
         nc.scalar.activation(out=root[:], in_=den[:], func=ACT.Abs_reciprocal_sqrt, bias=0.1)
         nc.scalar.activation(out=inv[:], in_=root[:], func=ACT.Square)
-        quantise_xq(3)
+        sum_folded(num, 0, 0)
+        fold(gated, 1, 0)
         value(3)
-        sum_folded(num, 0, TILES)
-        value(4)
-        fold(gated, 4, TILES + 4)
-        sum_folded(num, 1, TILES + 1)
-        value(5)
-        sum_folded(num, 4, TILES + 4)
-        sum_whole(num, gated, 5)
+        value_xt(4)
+        value_xt(5)
+        value_xq(4)
+        fold(gated, 4, 5)
+        sum_folded(num, 1, 0)
+        value_xq(5)
+        fold(gated, 5, 3)
         value(6)
-        nc.vector.tensor_tensor(out=mean[:], in0=num[:], in1=inv[:, :SUMMED, :], op=ALU.mult)
+        sum_folded(num, 4, 5)
         value(7)
+        divide(0)
+        sum_folded(num, 5, 3)
+        divide(1)
         for m in range(SUMMED, N_TILES):
             nc.tensor.transpose(banks[0][:, m * P : (m + 1) * P], inv[:, m, :], ident[:])
-        for m in range(SUMMED):
-            nc.tensor.transpose(banks[0][:, m * P : (m + 1) * P], mean[:, m, :], ident[:])
-        nc.scalar.copy(out=inv_rows[:], in_=banks[0][:, SUMMED * P :])
-        nc.scalar.activation(
-            out=dealt(0, SUMMED), in_=deal(banks[0][:, : SUMMED * P]), func=ACT.Copy, scale=bw_col[:]
+        nc.scalar.activation(out=factor_rows[:], in_=banks[0][:, SUMMED * P :], func=ACT.Copy, scale=bw_col[:])
+        stack_sum(banks[1], 2)
+        finish_mean(banks[3], 0)
+        finish_stack(banks[1], 2)
+        stack_sum(banks[2], 3)
+        finish_mean(banks[0], 1)
+        finish_stack(banks[2], 3)
+        store_rows(banks[6], 0)
+        pairs = y_pairs[:].rearrange("b u p e -> b u (p e)").bitcast(F32)
+        for u in range(2):
+            nc.tensor.transpose(banks[4][:, u * B : (u + 1) * B], pairs[:, u, :], ident[:])
+        store_rows(banks[5], 1)
+        nc.vector.tensor_copy(
+            out=y_bf[:].rearrange("p b r -> p (b r)").bitcast(F32).rearrange("p (b u) -> p b u", u=2),
+            in_=banks[4][:, : 2 * B].rearrange("p (u b) -> p b u", u=2),
         )
-        for m in range(SUMMED, N_TILES):
-            stack_sum(banks[m - 1], m)
-
-        for bank in (banks[3], banks[4]):
-            for i in range(PACK):
-                nc.tensor.transpose(bank[:, i * B : (i + 1) * B], y_rows[:, i, :], ident[:])
-        nc.vector.tensor_copy(out=y_bf[:], in_=banks[3][:].rearrange("p (i b) -> p b i", i=PACK))
-        nc.scalar.copy(out=y[:], in_=banks[4][:])
-        nc.sync.dma_start(out=out_0.rearrange("(p i) b -> p (i b)", i=PACK), in_=y[:])
         nc.vector.quantize_mx(
             out=y_w[:].bitcast(FP8X4), scales=y_s[:], in_=y_bf[:].rearrange("p b r -> p (b r)")
         )

@@ -56,7 +56,8 @@ def tile_mix_gated_mean_of_neighbours_pl_kernel(
         wv_s = sbuf("wv_s", [P, K_PASSES, N], U8)
         wq_s = sbuf("wq_s", [P, 1, N], U8)
         xq_raw = [sbuf("xq_raw%d" % q, [P, PACK, T_QUARTER], F32) for q in range(QUARTERS)]
-        xq_bf = [sbuf("xq_bf%d" % h, [P, T_HALF, PACK], BF16) for h in range(HALVES)]
+        stage = [sbuf("stage%d" % h, [P, 2 * T_HALF], F32) for h in range(HALVES)]
+        xq_bf = [stage[h][:].bitcast(BF16).rearrange("p (t j) -> p t j", j=PACK) for h in range(HALVES)]
         xq_w = [sbuf("xq_w%d" % h, [P, T_HALF], U32) for h in range(HALVES)]
         xq_s = [sbuf("xq_s%d" % h, [P, T_HALF], U8) for h in range(HALVES)]
         bw_col = sbuf("bw_col", [B, 1], F32)
@@ -64,7 +65,7 @@ def tile_mix_gated_mean_of_neighbours_pl_kernel(
         gates = [sbuf("gates%d" % k, [P, T_HALF], F32) for k in range(TILES)]
         gated = {k: sbuf("gated%d" % k, [P, T_HALF], F32) for k in range(TILES) if k % N_TILES < SUMMED}
         stacked = {m: sbuf("stacked%d" % m, [P, GROUP, B], F32) for m in range(SUMMED, N_TILES)}
-        folded = [sbuf("folded%d" % k, [P, T_HALF // 2], F32) for k in range(2 * TILES)]
+        folded = [stage[s // 4][:, (s % 4) * 256 : (s % 4 + 1) * 256] for s in range(8)]
         den = sbuf("den", [P, N_TILES, B], F32)
         num = sbuf("num", [P, SUMMED, B], F32)
         root = sbuf("root", [P, N_TILES, B], F32)
@@ -83,8 +84,8 @@ def tile_mix_gated_mean_of_neighbours_pl_kernel(
 
         def load_scales(queue, plane, scales, quad):
             queue.dma_start(
-                out=plane[32 * quad : 32 * quad + 4, :, :].bitcast(I32),
-                in_=scales[:, 4 * quad : 4 * quad + 4, :].rearrange("z r c -> r z c").bitcast(I32),
+                out=plane[quad:P:32, :, :].bitcast(I32),
+                in_=scales[:, quad:16:4, :].rearrange("z q c -> q z c").bitcast(I32),
             )
 
         xq_rows = xq.rearrange("(p j) t -> p j t", j=PACK)
@@ -92,7 +93,7 @@ def tile_mix_gated_mean_of_neighbours_pl_kernel(
         def load_xq(q):
             nc.sync.dma_start(out=xq_raw[q][:], in_=xq_rows[:, :, q * T_QUARTER : (q + 1) * T_QUARTER])
 
-        for plane in (wg_s, xt_s, wq_s, wv_s):
+        for plane in (xt_s, wg_s, wq_s, wv_s):
             nc.vector.memset(flat_words(plane), 0)
         warm = sbuf("warm", [P, 2], F32)
         nc.vector.memset(warm[:, 0:1], 0.0)
@@ -105,12 +106,10 @@ def tile_mix_gated_mean_of_neighbours_pl_kernel(
         nc.gpsimd.dma_start(out=wg_w[:].bitcast(I32), in_=wg_words.rearrange("z p c -> p z c").bitcast(I32))
         for quad in range(QUADS):
             load_scales(nc.gpsimd, wq_s, wq_scales, quad)
-        for quad in range(2):
-            load_scales(nc.sync, wg_s, wg_scales, quad)
         load_xt(0)
         for quad in range(QUADS):
             load_scales(nc.sync, xt_s, xt_scales, quad)
-        for quad in range(2, QUADS):
+        for quad in range(QUADS):
             load_scales(nc.sync, wg_s, wg_scales, quad)
         load_xq(0)
         load_xq(1)
@@ -126,17 +125,19 @@ def tile_mix_gated_mean_of_neighbours_pl_kernel(
         nc.sync.dma_start(out=bw_col[:], in_=bw.rearrange("o b -> b o"))
         make_identity(nc, ident[:])
 
-        def round_xq(q, copy):
+        def round_xq(q, copy, t0=0, t1=T_QUARTER):
+            first = (q % 2) * T_QUARTER
             copy(
-                out=xq_bf[q // 2][:, (q % 2) * T_QUARTER : (q % 2 + 1) * T_QUARTER, :].rearrange(
-                    "p (c i) j -> p c j i", i=4
-                ),
-                in_=xq_raw[q][:].rearrange("p j (c i) -> p c j i", i=4),
+                out=xq_bf[q // 2][:, first + t0 : first + t1, :],
+                in_=xq_raw[q][:, :, t0:t1].rearrange("p j t -> p t j"),
             )
+
+        def gpsimd_copy(out, in_):
+            nc.gpsimd.tensor_scalar(out=out, in0=in_, scalar1=1.0, scalar2=0.0, op0=ALU.mult, op1=ALU.add)
 
         def quantise_xq(h):
             nc.vector.quantize_mx(
-                out=xq_w[h][:].bitcast(FP8X4), scales=xq_s[h][:], in_=xq_bf[h][:].rearrange("p t j -> p (t j)")
+                out=xq_w[h][:].bitcast(FP8X4), scales=xq_s[h][:], in_=stage[h][:].bitcast(BF16)
             )
 
         def bank_order(k):
@@ -169,6 +170,13 @@ def tile_mix_gated_mean_of_neighbours_pl_kernel(
                     stop=(z == K_PASSES - 1),
                 )
             nc.scalar.activation(out=tile_order(gates[k], k), in_=bank_order(k), func=ACT.Sigmoid)
+
+        def warm_up():
+            codes, scales = xt_operand(0, 0)
+            nc.tensor.matmul_mx(
+                out=banks[TILES - 1][:], lhsT=xt_w[0][:, 0, : 2 * P].bitcast(FP4X4), lhsT_scale=xt_s[:, 0, :P],
+                rhs=codes, rhs_scale=scales, start=True, stop=True,
+            )
 
         def value_xt(k):
             h, m = divmod(k, N_TILES)
@@ -221,14 +229,14 @@ def tile_mix_gated_mean_of_neighbours_pl_kernel(
 
         def fold(terms, k, slot):
             nc.gpsimd.tensor_tensor(
-                out=folded[slot][:], in0=terms[k][:, : T_HALF // 2], in1=terms[k][:, T_HALF // 2 :], op=ALU.add
+                out=folded[slot], in0=terms[k][:, : T_HALF // 2], in1=terms[k][:, T_HALF // 2 :], op=ALU.add
             )
 
         def sum_folded(total, k, slot):
             pattern = "p (b j) -> p b j" if k % N_TILES < SUMMED else "p (j b) -> p b j"
             nc.vector.tensor_reduce(
                 out=groups(total, k),
-                in_=folded[slot][:].rearrange(pattern, j=GROUP // 2),
+                in_=folded[slot].rearrange(pattern, j=GROUP // 2),
                 axis=AXIS.X,
                 op=ALU.add,
             )
@@ -269,53 +277,56 @@ def tile_mix_gated_mean_of_neighbours_pl_kernel(
         def divide(m):
             nc.vector.tensor_tensor(out=mean[:, m, :], in0=num[:, m, :], in1=inv[:, m, :], op=ALU.mult)
 
+        warm_up()
+        warm_up()
         round_xq(0, nc.vector.tensor_copy)
         gate(0)
         sum_whole(den, gates, 0)
         round_xq(1, nc.vector.tensor_copy)
+        quantise_xq(0)
         gate(1)
         sum_whole(den, gates, 1)
-        quantise_xq(0)
         gate(2)
-        fold(gates, 2, 2)
+        fold(gates, 2, 0)
         gate(3)
-        fold(gates, 3, 3)
+        fold(gates, 3, 1)
         gate(4)
         sum_whole(den, gates, 4)
         gate(5)
-        sum_folded(den, 2, 2)
         sum_whole(den, gates, 5)
         gate(6)
-        fold(gates, 6, 6)
+        fold(gates, 6, 2)
         gate(7)
-        fold(gates, 7, 7)
-        sum_folded(den, 3, 3)
+        fold(gates, 7, 3)
         round_xq(2, nc.scalar.copy)
-        round_xq(3, nc.scalar.copy)
+        round_xq(3, nc.scalar.copy, 0, T_QUARTER // 2)
+        round_xq(3, gpsimd_copy, T_QUARTER // 2, T_QUARTER)
+        sum_folded(den, 2, 0)
         value(0)
-        fold(gated, 0, 0)
-        sum_folded(den, 6, 6)
+        sum_folded(den, 3, 1)
         value(1)
-        sum_folded(den, 7, 7)
+        sum_folded(den, 6, 2)
         value(2)
         quantise_xq(1)
+        fold(gated, 0, 4)
+        fold(gated, 1, 5)
+        sum_folded(den, 7, 3)
         nc.scalar.activation(out=root[:], in_=den[:], func=ACT.Abs_reciprocal_sqrt, bias=0.1)
         nc.scalar.activation(out=inv[:], in_=root[:], func=ACT.Square)
-        sum_folded(num, 0, 0)
-        fold(gated, 1, 0)
         value(3)
         value_xt(4)
         value_xt(5)
         value_xq(4)
-        fold(gated, 4, 5)
-        sum_folded(num, 1, 0)
+        fold(gated, 4, 6)
+        sum_folded(num, 0, 4)
         value_xq(5)
-        fold(gated, 5, 3)
+        fold(gated, 5, 7)
+        sum_folded(num, 1, 5)
         value(6)
-        sum_folded(num, 4, 5)
+        sum_folded(num, 4, 6)
         value(7)
         divide(0)
-        sum_folded(num, 5, 3)
+        sum_folded(num, 5, 7)
         divide(1)
         for m in range(SUMMED, N_TILES):
             nc.tensor.transpose(banks[0][:, m * P : (m + 1) * P], inv[:, m, :], ident[:])

from contextlib import ExitStack

import concourse.mybir as mybir
from concourse.masks import make_identity

K, L, T, B, N = 1024, 512, 1024, 128, 512
FLOPS = 2 * N * T * (K + L + K)

F32 = mybir.dt.float32
BF16 = mybir.dt.bfloat16
I32 = mybir.dt.int32
U32 = mybir.dt.uint32
U8 = mybir.dt.uint8
FP8X4 = mybir.dt.float8_e4m3fn_x4
FP4X4 = mybir.dt.float4_e2m1fn_x4
ACT = mybir.ActivationFunctionType
ALU = mybir.AluOpType
AXIS = mybir.AxisListType

P = 128
PACK = 4
K_PASSES = K // (P * PACK)
GROUP = T // B
N_TILES = N // P
HALVES = 2
T_HALF = T // HALVES
B_HALF = B // HALVES
QUARTERS = 4
T_QUARTER = T // QUARTERS
TILES = HALVES * N_TILES
QUADS = 4
SUMMED = 2


def tile_mix_gated_mean_of_neighbours_pl_kernel(
    tc, xt_words, xt_scales, wv_words, wv_scales, xq, wq_words, wq_scales, wg_words, wg_scales, bw,
    out_0, out_1, out_2,
):
    nc = tc.nc
    with ExitStack() as ctx:
        sb = ctx.enter_context(tc.tile_pool(name="sb", bufs=1))
        ps = ctx.enter_context(tc.psum_pool(name="ps", bufs=1))
        ctx.enter_context(tc.manual_schedule())

        def sbuf(name, shape, dtype):
            return sb.tile(shape, dtype, name=name, align_bytes=64)

        banks = [ps.tile([P, T_HALF], F32, name="bank%d" % k) for k in range(TILES)]

        xt_w = [sbuf("xt_w%d" % h, [P, K_PASSES, 2 * T_HALF], U8) for h in range(HALVES)]
        wg_w = sbuf("wg_w", [P, K_PASSES, 2 * N], U8)
        wv_w = sbuf("wv_w", [P, K_PASSES, N], U32)
        wq_w = sbuf("wq_w", [P, N], U32)
        xt_s = sbuf("xt_s", [P, K_PASSES, T], U8)
        wg_s = sbuf("wg_s", [P, K_PASSES, N], U8)
        wv_s = sbuf("wv_s", [P, K_PASSES, N], U8)
        wq_s = sbuf("wq_s", [P, 1, N], U8)
        xq_raw = [sbuf("xq_raw%d" % q, [P, PACK, T_QUARTER], F32) for q in range(QUARTERS)]
        stage = [sbuf("stage%d" % h, [P, 2 * T_HALF], F32) for h in range(HALVES)]
        xq_bf = [stage[h][:].bitcast(BF16).rearrange("p (t j) -> p t j", j=PACK) for h in range(HALVES)]
        xq_w = [sbuf("xq_w%d" % h, [P, T_HALF], U32) for h in range(HALVES)]
        xq_s = [sbuf("xq_s%d" % h, [P, T_HALF], U8) for h in range(HALVES)]
        bw_col = sbuf("bw_col", [B, 1], F32)
        ident = sbuf("ident", [P, P], F32)
        gates = [sbuf("gates%d" % k, [P, T_HALF], F32) for k in range(TILES)]
        gated = {k: sbuf("gated%d" % k, [P, T_HALF], F32) for k in range(TILES) if k % N_TILES < SUMMED}
        stacked = {m: sbuf("stacked%d" % m, [P, GROUP, B], F32) for m in range(SUMMED, N_TILES)}
        folded = [stage[s // 4][:, (s % 4) * 256 : (s % 4 + 1) * 256] for s in range(8)]
        den = sbuf("den", [P, N_TILES, B], F32)
        num = sbuf("num", [P, SUMMED, B], F32)
        root = sbuf("root", [P, N_TILES, B], F32)
        inv = sbuf("inv", [P, N_TILES, B], F32)
        mean = sbuf("mean", [P, SUMMED, B], F32)
        factor_rows = sbuf("factor_rows", [B, (N_TILES - SUMMED) * P], F32)
        y_rows = sbuf("y_rows", [B, N], F32)
        y_pairs = sbuf("y_pairs", [B, 2, P, 2], BF16)
        y = sbuf("y", [P, 2, 2 * B], F32)
        y_bf = sbuf("y_bf", [P, B, PACK], BF16)
        y_w = sbuf("y_w", [P, B], U32)
        y_s = sbuf("y_s", [P, B], U8)

        def flat_words(plane):
            return plane[:].rearrange("p z c -> p (z c)").bitcast(I32)

        def load_scales(queue, plane, scales, quad):
            queue.dma_start(
                out=plane[quad:P:32, :, :].bitcast(I32),
                in_=scales[:, quad:16:4, :].rearrange("z q c -> q z c").bitcast(I32),
            )

        xq_rows = xq.rearrange("(p j) t -> p j t", j=PACK)

        def load_xq(q):
            nc.sync.dma_start(out=xq_raw[q][:], in_=xq_rows[:, :, q * T_QUARTER : (q + 1) * T_QUARTER])

        for plane in (xt_s, wg_s, wq_s, wv_s):
            nc.vector.memset(flat_words(plane), 0)
        warm = sbuf("warm", [P, 2], F32)
        nc.vector.memset(warm[:, 0:1], 0.0)
        nc.scalar.activation(out=warm[:, 1:2], in_=warm[:, 0:1], func=ACT.Sigmoid)

        def load_xt(h):
            cols = slice(2 * h * T_HALF, 2 * (h + 1) * T_HALF)
            nc.sync.dma_start(out=xt_w[h][:].bitcast(I32), in_=xt_words.rearrange("z p c -> p z c")[:, :, cols].bitcast(I32))

        nc.gpsimd.dma_start(out=wg_w[:].bitcast(I32), in_=wg_words.rearrange("z p c -> p z c").bitcast(I32))
        for quad in range(QUADS):
            load_scales(nc.gpsimd, wq_s, wq_scales, quad)
        load_xt(0)
        for quad in range(QUADS):
            load_scales(nc.sync, xt_s, xt_scales, quad)
        for quad in range(QUADS):
            load_scales(nc.sync, wg_s, wg_scales, quad)
        load_xq(0)
        load_xq(1)
        load_xt(1)
        nc.sync.dma_start(
            out=wv_w[:].bitcast(I32), in_=wv_words.rearrange("z p n r -> p z (n r)").bitcast(I32)
        )
        for quad in range(QUADS):
            load_scales(nc.sync, wv_s, wv_scales, quad)
        nc.sync.dma_start(out=wq_w[:].bitcast(I32), in_=wq_words[0].rearrange("p n r -> p (n r)").bitcast(I32))
        load_xq(2)
        load_xq(3)
        nc.sync.dma_start(out=bw_col[:], in_=bw.rearrange("o b -> b o"))
        make_identity(nc, ident[:])

        def round_xq(q, copy, t0=0, t1=T_QUARTER):
            first = (q % 2) * T_QUARTER
            copy(
                out=xq_bf[q // 2][:, first + t0 : first + t1, :],
                in_=xq_raw[q][:, :, t0:t1].rearrange("p j t -> p t j"),
            )

        def gpsimd_copy(out, in_):
            nc.gpsimd.tensor_scalar(out=out, in0=in_, scalar1=1.0, scalar2=0.0, op0=ALU.mult, op1=ALU.add)

        def quantise_xq(h):
            nc.vector.quantize_mx(
                out=xq_w[h][:].bitcast(FP8X4), scales=xq_s[h][:], in_=stage[h][:].bitcast(BF16)
            )

        def bank_order(k):
            if k % N_TILES < SUMMED:
                return banks[k][:].rearrange("p (b u j) -> p u b j", u=2, j=GROUP // 2)
            return banks[k][:].rearrange("p (b j) -> p j b", j=GROUP)

        def tile_order(t, k):
            if k % N_TILES < SUMMED:
                return t[:].rearrange("p (u b j) -> p u b j", u=2, j=GROUP // 2)
            return t[:].rearrange("p (j b) -> p j b", j=GROUP)

        def xt_operand(z, h):
            return (
                xt_w[h][:, z, :].bitcast(FP4X4),
                xt_s[:, z, h * T_HALF : (h + 1) * T_HALF],
            )

        def gate(k):
            h, m = divmod(k, N_TILES)
            for z in range(K_PASSES):
                codes, scales = xt_operand(z, h)
                nc.tensor.matmul_mx(
                    out=banks[k][:],
                    lhsT=wg_w[:, z, 2 * m * P : 2 * (m + 1) * P].bitcast(FP4X4),
                    lhsT_scale=wg_s[:, z, m * P : (m + 1) * P],
                    rhs=codes,
                    rhs_scale=scales,
                    start=(z == 0),
                    stop=(z == K_PASSES - 1),
                )
            nc.scalar.activation(out=tile_order(gates[k], k), in_=bank_order(k), func=ACT.Sigmoid)

        def warm_up():
            codes, scales = xt_operand(0, 0)
            nc.tensor.matmul_mx(
                out=banks[TILES - 1][:], lhsT=xt_w[0][:, 0, : 2 * P].bitcast(FP4X4), lhsT_scale=xt_s[:, 0, :P],
                rhs=codes, rhs_scale=scales, start=True, stop=True,
            )

        def value_xt(k):
            h, m = divmod(k, N_TILES)
            cols = slice(m * P, (m + 1) * P)
            for z in range(K_PASSES):
                codes, scales = xt_operand(z, h)
                nc.tensor.matmul_mx(
                    out=banks[k][:],
                    lhsT=wv_w[:, z, cols].bitcast(FP8X4),
                    lhsT_scale=wv_s[:, z, cols],
                    rhs=codes,
                    rhs_scale=scales,
                    start=(z == 0),
                    stop=False,
                )

        def value_xq(k):
            h, m = divmod(k, N_TILES)
            cols = slice(m * P, (m + 1) * P)
            nc.tensor.matmul_mx(
                out=banks[k][:],
                lhsT=wq_w[:, cols].bitcast(FP8X4),
                lhsT_scale=wq_s[:, 0, cols],
                rhs=xq_w[h][:].bitcast(FP8X4),
                rhs_scale=xq_s[h][:],
                start=False,
                stop=True,
            )
            if m < SUMMED:
                products = tile_order(gated[k], k)
            else:
                products = stacked[m][:, :, h * B_HALF : (h + 1) * B_HALF]
            nc.vector.tensor_tensor(out=products, in0=bank_order(k), in1=tile_order(gates[k], k), op=ALU.mult)

        def value(k):
            value_xt(k)
            value_xq(k)

        def groups(total, k):
            h, m = divmod(k, N_TILES)
            return total[:, m, h * B_HALF : (h + 1) * B_HALF]

        def sum_whole(total, terms, k):
            nc.vector.tensor_reduce(
                out=groups(total, k),
                in_=terms[k][:].rearrange("p (u b j) -> p b u j", u=2, j=GROUP // 2),
                axis=AXIS.XY,
                op=ALU.add,
            )

        def fold(terms, k, slot):
            nc.gpsimd.tensor_tensor(
                out=folded[slot], in0=terms[k][:, : T_HALF // 2], in1=terms[k][:, T_HALF // 2 :], op=ALU.add
            )

        def sum_folded(total, k, slot):
            pattern = "p (b j) -> p b j" if k % N_TILES < SUMMED else "p (j b) -> p b j"
            nc.vector.tensor_reduce(
                out=groups(total, k),
                in_=folded[slot].rearrange(pattern, j=GROUP // 2),
                axis=AXIS.X,
                op=ALU.add,
            )

        def dealt(m0, m1):
            return y_pairs[:, :, 32 * m0 : 32 * m1, :]

        def deal(ap):
            return ap.rearrange("b (p u e) -> b u p e", u=2, e=2)

        def stack_sum(bank, m):
            for j in range(GROUP):
                nc.tensor.matmul(
                    out=bank[:, :P], lhsT=stacked[m][:, j, :], rhs=ident[:], is_transpose=True,
                    start=(j == 0), stop=(j == GROUP - 1),
                )

        def finish_stack(bank, m):
            factor = factor_rows[:, (m - SUMMED) * P : (m - SUMMED + 1) * P]
            nc.vector.tensor_tensor(out=dealt(m, m + 1), in0=deal(bank[:, :P]), in1=deal(factor), op=ALU.mult)
            nc.vector.tensor_tensor(out=y_rows[:, m * P : (m + 1) * P], in0=bank[:, :P], in1=factor, op=ALU.mult)

        def finish_mean(bank, m):
            nc.tensor.transpose(bank[:, :P], mean[:, m, :], ident[:])
            nc.scalar.activation(out=dealt(m, m + 1), in_=deal(bank[:, :P]), func=ACT.Copy, scale=bw_col[:])
            nc.scalar.activation(out=y_rows[:, m * P : (m + 1) * P], in_=bank[:, :P], func=ACT.Copy, scale=bw_col[:])

        def store_rows(bank, first):
            for slot in range(2):
                m = first + 2 * slot
                nc.tensor.transpose(bank[:, slot * B : (slot + 1) * B], y_rows[:, m * P : (m + 1) * P], ident[:])
            nc.scalar.copy(out=y[:, first, :], in_=bank[:, : 2 * B])
            nc.scalar.dma_start(
                out=out_0.rearrange("(s f p) b -> p f s b", s=2, p=P)[:, first, :, :],
                in_=y[:, first, :].rearrange("p (s b) -> p s b", s=2),
            )

        def divide(m):
            nc.vector.tensor_tensor(out=mean[:, m, :], in0=num[:, m, :], in1=inv[:, m, :], op=ALU.mult)

        warm_up()
        warm_up()
        round_xq(0, nc.vector.tensor_copy)
        gate(0)
        sum_whole(den, gates, 0)
        round_xq(1, nc.vector.tensor_copy)
        quantise_xq(0)
        gate(1)
        sum_whole(den, gates, 1)
        gate(2)
        fold(gates, 2, 0)
        gate(3)
        fold(gates, 3, 1)
        gate(4)
        sum_whole(den, gates, 4)
        gate(5)
        sum_whole(den, gates, 5)
        gate(6)
        fold(gates, 6, 2)
        gate(7)
        fold(gates, 7, 3)
        round_xq(2, nc.scalar.copy)
        round_xq(3, nc.scalar.copy, 0, T_QUARTER // 2)
        round_xq(3, gpsimd_copy, T_QUARTER // 2, T_QUARTER)
        sum_folded(den, 2, 0)
        value(0)
        sum_folded(den, 3, 1)
        value(1)
        sum_folded(den, 6, 2)
        value(2)
        quantise_xq(1)
        fold(gated, 0, 4)
        fold(gated, 1, 5)
        sum_folded(den, 7, 3)
        nc.scalar.activation(out=root[:], in_=den[:], func=ACT.Abs_reciprocal_sqrt, bias=0.1)
        nc.scalar.activation(out=inv[:], in_=root[:], func=ACT.Square)
        value(3)
        value_xt(4)
        value_xt(5)
        value_xq(4)
        fold(gated, 4, 6)
        sum_folded(num, 0, 4)
        value_xq(5)
        fold(gated, 5, 7)
        sum_folded(num, 1, 5)
        value(6)
        sum_folded(num, 4, 6)
        value(7)
        divide(0)
        sum_folded(num, 5, 7)
        divide(1)
        for m in range(SUMMED, N_TILES):
            nc.tensor.transpose(banks[0][:, m * P : (m + 1) * P], inv[:, m, :], ident[:])
        nc.scalar.activation(out=factor_rows[:], in_=banks[0][:, SUMMED * P :], func=ACT.Copy, scale=bw_col[:])
        stack_sum(banks[1], 2)
        finish_mean(banks[3], 0)
        finish_stack(banks[1], 2)
        stack_sum(banks[2], 3)
        finish_mean(banks[0], 1)
        finish_stack(banks[2], 3)
        store_rows(banks[6], 0)
        pairs = y_pairs[:].rearrange("b u p e -> b u (p e)").bitcast(F32)
        for u in range(2):
            nc.tensor.transpose(banks[4][:, u * B : (u + 1) * B], pairs[:, u, :], ident[:])
        store_rows(banks[5], 1)
        nc.vector.tensor_copy(
            out=y_bf[:].rearrange("p b r -> p (b r)").bitcast(F32).rearrange("p (b u) -> p b u", u=2),
            in_=banks[4][:, : 2 * B].rearrange("p (u b) -> p b u", u=2),
        )
        nc.vector.quantize_mx(
            out=y_w[:].bitcast(FP8X4), scales=y_s[:], in_=y_bf[:].rearrange("p b r -> p (b r)")
        )
        nc.sync.dma_start(out=out_1[0].rearrange("p c r -> p (c r)").bitcast(I32), in_=y_w[:].bitcast(I32))
        for quad in range(QUADS):
            queue = nc.scalar if quad % 2 == 0 else nc.sync
            queue.dma_start(
                out=out_2[0, 4 * quad : 4 * quad + 4, :].bitcast(I32),
                in_=y_s[32 * quad : 32 * quad + 4, :].bitcast(I32),
            )
